import numpy as np
import ml_dtypes


def mxq(x, axis, fmt="e4m3"):
    dtype, down = {"e4m3": (ml_dtypes.float8_e4m3fn, 7), "e5m2": (ml_dtypes.float8_e5m2, 14)}[fmt]
    v = np.moveaxis(np.asarray(x, np.float32).astype(ml_dtypes.bfloat16).astype(np.float64), axis, -1)
    blocks = v.reshape(v.shape[:-1] + (-1, 32))
    amax = np.abs(blocks).max(-1, keepdims=True)
    byte = np.maximum(np.where(amax > 0, np.frexp(amax)[1] - 1 + 127, 0) - down, 1)
    scale = np.exp2(byte - 127.0)
    codes = (blocks / scale).astype(np.float32).astype(dtype).astype(np.float64)
    return np.moveaxis((codes * scale).reshape(v.shape), -1, axis)


WIDE = False


def mx_kscale(k, group=512):
    if not WIDE:
        return np.ones(k)
    levels = np.array([10, -10, 5, -5, 0])
    if group != 512:
        return np.exp2(np.random.permutation(np.resize(levels, k // group))).repeat(group)
    if k % 512:
        return np.exp2(np.random.permutation(np.resize(levels, k // 32))).repeat(32)
    a = np.empty((k // 512, 16))
    for p in range(k // 512):
        a[p, :8] = np.random.permutation(np.resize(levels, 8))
        for g in range(8):
            far = levels[np.abs(levels - a[p, g]) >= 10]
            a[p, g + 8] = far[np.random.randint(len(far))]
    return np.exp2(a.ravel()).repeat(32)


def f64(x):
    return np.asarray(x).astype(np.float64)


def striped(idx):
    return np.tile(np.asarray(idx).reshape(-1, 16).T, (8, 1)).astype(np.uint16)


def unstriped(offs):
    return offs[:16].T.reshape(-1).astype(np.int64)


H, KV, D, NQ, N = 8, 8, 128, 512, 512
CAP = 2.0


def setup_inputs():
    n = np.random.standard_normal
    s = mx_kscale(D, 0)[:, None]
    u = mx_kscale(N)
    t = np.random.uniform(0.5, 2.0, N) * u
    v = n((KV, N, 128))
    v[:, :, 127] = 1.0
    return {
        "qT": (n((H, D, NQ)) * s * (0.70 / np.sqrt(D))).astype(np.float32),
        "kT": (n((KV, D, N)) / s).astype(np.float32),
        "t": t.reshape(N, 1).astype(np.float32),
        "v": (v / t[:, None]).astype(np.float32),
        "mask": (np.arange(N)[:, None] <= np.sort(np.random.randint(N // 4, N, NQ))[None, :]).astype(np.float32),
        "og": n((H, NQ, 128)).astype(np.float32),
    }


def reference(qT, kT, t, v, mask, og):
    a = mxq(f64(kT), 1, "e4m3").transpose(0, 2, 1) @ mxq(f64(qT), 1, "e4m3")
    a = CAP * np.tanh(a / CAP)
    p = np.exp(a)
    p = p * f64(mask)
    w = p * f64(t)
    y = mxq(w, 1, "e4m3").transpose(0, 2, 1) @ mxq(f64(v), 1, "e4m3")
    y = y / (y[:, :, 127:128])
    y = y / (1.0 + np.exp(-f64(og)))
    return y

@@ -1,0 +1,314 @@
+from contextlib import ExitStack
+
+import concourse.mybir as mybir
+
+H, D, NQ, N = 8, 128, 512, 512
+CAP = 2.0
+FLOPS = 2 * 2 * H * NQ * N * D
+
+F32 = mybir.dt.float32
+BF16 = mybir.dt.bfloat16
+U32 = mybir.dt.uint32
+U8 = mybir.dt.uint8
+FP8X4 = mybir.dt.float8_e4m3fn_x4
+ACT = mybir.ActivationFunctionType
+ALU = mybir.AluOpType
+
+P = 128
+PACK = 4
+ROWS = D // PACK
+SET = P // ROWS
+QT = 128
+TILES = NQ // QT
+STEPS = (H // SET) * TILES
+UNITS = STEPS * SET
+PAIRS = UNITS // 2
+W = QT * PACK
+HALF = N // 2
+
+
+def tile_rows_a_exp_mask_cap_gate_kernel(tc, qT, kT, t, v, mask, og, out):
+    nc = tc.nc
+    with ExitStack() as ctx:
+        keep = ctx.enter_context(tc.tile_pool(name="keep", bufs=1))
+        flow = ctx.enter_context(tc.tile_pool(name="flow", bufs=3))
+        psum = ctx.enter_context(tc.psum_pool(name="psum", bufs=1))
+        ctx.enter_context(tc.manual_schedule())
+
+        def kept(name, shape, dtype):
+            return keep.tile(shape, dtype, name=name, align_bytes=64)
+
+        def load(name, src):
+            dst = kept(name, list(src.shape), F32)
+            nc.sync.dma_start(out=dst[:], in_=src)
+            return dst
+
+        def load_features(name, x, a, c0, c1):
+            return load(name, x[SET * a : SET * (a + 1), :, c0:c1].rearrange("h (p j) n -> (h p) j n", j=PACK))
+
+        def load_mask(name, c0, c1):
+            return load(name, mask[:, c0:c1].rearrange("(p j) q -> p j q", j=PACK))
+
+        def load_values(a, u):
+            h0 = SET * a + 2 * u
+            return load("v_raw%d_%d" % (a, u), v[h0 : h0 + 2].rearrange("h (p j) e -> p h (j e)", j=PACK))
+
+        def rows_of(x, s, g0, g1):
+            a, c = divmod(s, TILES)
+            return x[SET * a + g0 : SET * a + g1, QT * c : QT * (c + 1), :].rearrange("h q e -> q h e")
+
+        def load_gate(s):
+            return load("og%d" % s, rows_of(og, s, 0, SET))
+
+        q_raw, k_raw, v_raw, og_raw, m_raw = {}, {}, {}, {}, {}
+        q_raw[0] = load_features("q_raw0", qT, 0, 0, QT)[:]
+        k_raw[0, 0] = load_features("k_raw00", kT, 0, 0, HALF)[:]
+        k_raw[0, 1] = load_features("k_raw01", kT, 0, HALF, N)[:]
+        q_raw[1] = load_features("q_raw1", qT, 0, QT, 2 * QT)[:]
+        m_raw[0] = load_mask("m_raw0", 0, QT)[:]
+        t_sb = load("t_sb", t.rearrange("(p j) o -> p (j o)", j=PACK))
+        v_raw[0, 0] = load_values(0, 0)
+        v_raw[0, 1] = load_values(0, 1)
+        q23 = load_features("q_raw23", qT, 0, 2 * QT, NQ)
+        q_raw[2], q_raw[3] = q23[:, :, 0:QT], q23[:, :, QT : 2 * QT]
+        m123 = load_mask("m_raw123", QT, NQ)
+        for c in range(1, TILES):
+            m_raw[c] = m123[:, :, QT * (c - 1) : QT * c]
+        og_raw[0] = load_gate(0)
+        k1 = load_features("k_raw1", kT, 1, 0, N)
+        k_raw[1, 0], k_raw[1, 1] = k1[:, :, 0:HALF], k1[:, :, HALF:N]
+        og_raw[1] = load_gate(1)
+        q1 = load_features("q_raw4567", qT, 1, 0, NQ)
+        for c in range(TILES):
+            q_raw[TILES + c] = q1[:, :, QT * c : QT * (c + 1)]
+        og_raw[2] = load_gate(2)
+        v_raw[1, 0] = load_values(1, 0)
+        v_raw[1, 1] = load_values(1, 1)
+        for s in range(3, STEPS):
+            og_raw[s] = load_gate(s)
+
+        k_bf = [kept("k_bf%d" % a, [P, N * PACK], BF16) for a in range(2)]
+        k_codes = [kept("k_codes%d" % a, [P, N], U32) for a in range(2)]
+        k_scales = [kept("k_scales%d" % a, [P, N], U8) for a in range(2)]
+        v_bf = [kept("v_bf%d" % a, [P, SET * W], BF16) for a in range(2)]
+        v_codes = [kept("v_codes%d" % a, [P, SET * D], U32) for a in range(2)]
+        v_scales = [kept("v_scales%d" % a, [P, SET * D], U8) for a in range(2)]
+        q_bf = [kept("q_bf%d" % s, [P, W], BF16) for s in range(STEPS)]
+        q_codes = [kept("q_codes%d" % s, [P, QT], U32) for s in range(STEPS)]
+        q_scales = [kept("q_scales%d" % s, [P, QT], U8) for s in range(STEPS)]
+        mask_t = [kept("mask_t%d" % c, [P, W], F32) for c in range(TILES)]
+        gate = [kept("gate%d" % s, [P, SET, D], F32) for s in range(STEPS)]
+        result = [kept("result%d" % s, [P, SET, D], F32) for s in range(STEPS)]
+        recip = [kept("recip%d" % s, [P, SET], F32) for s in range(STEPS)]
+        score_bank = [psum.tile([P, W], F32, name="score_bank%d" % g) for g in range(SET)]
+        y_bank = [psum.tile([P, SET, D], F32, name="y_bank%d" % b) for b in range(4)]
+        capped, weights, w_bf, w_codes, w_scales = {}, {}, {}, {}, {}
+
+        def quantize(codes, scales, values):
+            nc.vector.quantize_mx(out=codes.bitcast(FP8X4), scales=scales, in_=values)
+
+        def spread_q(s):
+            nc.vector.tensor_copy(
+                out=q_bf[s][:].rearrange("p (c i j) -> p c j i", i=4, j=PACK),
+                in_=q_raw[s].rearrange("p j (c i) -> p c j i", i=4),
+            )
+
+        def quant_q(s):
+            quantize(q_codes[s][:], q_scales[s][:], q_bf[s][:])
+
+        def spread_k(a, u, r0, r1):
+            s0, s1 = u * HALF // PACK, (u + 1) * HALF // PACK
+            nc.vector.tensor_copy(
+                out=k_bf[a][:].rearrange("p (r s j) -> p s j r", r=PACK, j=PACK)[:, s0:s1, :, r0:r1],
+                in_=k_raw[a, u].rearrange("p j (s r) -> p s j r", r=PACK)[:, :, :, r0:r1],
+            )
+
+        def quant_k(a, c0, c1):
+            quantize(k_codes[a][:, c0:c1], k_scales[a][:, c0:c1], k_bf[a][:, PACK * c0 : PACK * c1])
+
+        def quant_k_half(a, u):
+            for r in range(PACK):
+                quant_k(a, P * r + 64 * u, P * r + 64 * (u + 1))
+
+        def spread_v(a, u):
+            nc.vector.tensor_copy(
+                out=v_bf[a][:, 2 * W * u : 2 * W * (u + 1)].rearrange("p (h c i j) -> p h c j i", h=2, i=4, j=PACK),
+                in_=v_raw[a, u][:].rearrange("p h (j c i) -> p h c j i", j=PACK, i=4),
+            )
+
+        def quant_v(a):
+            quantize(v_codes[a][:], v_scales[a][:], v_bf[a][:])
+
+        def scale_mask(c):
+            nc.vector.tensor_tensor(
+                out=mask_t[c][:].rearrange("p (q j) -> p q j", j=PACK),
+                in0=m_raw[c].rearrange("p j q -> p q j"),
+                in1=t_sb[:].unsqueeze(1).to_broadcast([P, QT, PACK]),
+                op=ALU.mult,
+            )
+
+        def scores(n):
+            s, g = divmod(n, SET)
+            a = s // TILES
+            rows = slice(ROWS * g, ROWS * (g + 1))
+            for r in range(PACK):
+                cols = slice(P * r, P * (r + 1))
+                nc.tensor.matmul_mx(
+                    out=score_bank[g][:, cols],
+                    lhsT=k_codes[a][rows, cols].bitcast(FP8X4),
+                    lhsT_scale=k_scales[a][rows, cols],
+                    rhs=q_codes[s][rows, :].bitcast(FP8X4),
+                    rhs_scale=q_scales[s][rows, :],
+                    start=True,
+                    stop=True,
+                )
+
+        def cap(n):
+            m, i = divmod(n, 2)
+            if i == 0:
+                capped[m] = flow.tile([P, 2, W], F32, name="capped")
+            nc.scalar.activation(
+                out=capped[m][:, i, :].rearrange("p (q r) -> p q r", r=PACK),
+                in_=score_bank[n % SET][:].rearrange("p (r q) -> p q r", r=PACK),
+                func=ACT.Tanh,
+                scale=1.0 / CAP,
+            )
+            if n + SET < UNITS:
+                scores(n + SET)
+
+        def exponent(m, i0, i1):
+            if i0 == 0:
+                weights[m] = flow.tile([P, 2, W], F32, name="weights", bufs=4)
+            nc.scalar.activation(out=weights[m][:, i0:i1, :], in_=capped[m][:, i0:i1, :], func=ACT.Exp, scale=CAP)
+
+        def gate_tanh(s):
+            nc.scalar.activation(out=gate[s][:], in_=og_raw[s][:], func=ACT.Tanh, scale=0.5)
+
+        def weigh(m, i0, i1):
+            if i0 == 0:
+                w_bf[m] = flow.tile([P, 2 * W], BF16, name="w_bf", align_bytes=64)
+            c = (m // 2) % TILES
+            nc.vector.tensor_tensor(
+                out=w_bf[m][:, W * i0 : W * i1].rearrange("p (i x) -> p i x", x=W),
+                in0=weights[m][:, i0:i1, :],
+                in1=mask_t[c][:].unsqueeze(1).to_broadcast([P, i1 - i0, W]),
+                op=ALU.mult,
+            )
+
+        def quant_w(m, i0, i1):
+            if i0 == 0:
+                w_codes[m] = flow.tile([P, 2 * QT], U32, name="w_codes", align_bytes=64)
+                w_scales[m] = flow.tile([P, 2 * QT], U8, name="w_scales", align_bytes=64)
+            quantize(w_codes[m][:, QT * i0 : QT * i1], w_scales[m][:, QT * i0 : QT * i1], w_bf[m][:, W * i0 : W * i1])
+
+        def y_of(n):
+            s, g = divmod(n, SET)
+            bank = s % 4 if n < UNITS - 2 else n % 2
+            return y_bank[bank]
+
+        def attend(m, i0, i1):
+            for i in range(i0, i1):
+                n = 2 * m + i
+                s, g = divmod(n, SET)
+                a = s // TILES
+                nc.tensor.matmul_mx(
+                    out=y_of(n)[:, g, :],
+                    lhsT=w_codes[m][:, QT * i : QT * (i + 1)].bitcast(FP8X4),
+                    lhsT_scale=w_scales[m][:, QT * i : QT * (i + 1)],
+                    rhs=v_codes[a][:, D * g : D * (g + 1)].bitcast(FP8X4),
+                    rhs_scale=v_scales[a][:, D * g : D * (g + 1)],
+                    start=True,
+                    stop=True,
+                )
+
+        def gate_y(s, g0=0, g1=SET):
+            y = y_of(SET * s + g0)
+            nc.vector.reciprocal(out=recip[s][:, g0:g1], in_=y[:, g0:g1, D - 1])
+            nc.vector.scalar_tensor_tensor(
+                out=result[s][:, g0:g1, :],
+                in0=gate[s][:, g0:g1, :],
+                scalar=1.0,
+                in1=y[:, g0:g1, :],
+                op0=ALU.add,
+                op1=ALU.mult,
+            )
+
+        def finish(s, g0=0, g1=SET):
+            for g in range(g0, g1):
+                nc.vector.tensor_scalar(
+                    out=result[s][:, g, :],
+                    in0=result[s][:, g, :],
+                    scalar1=recip[s][:, g : g + 1],
+                    scalar2=0.5,
+                    op0=ALU.mult,
+                    op1=ALU.mult,
+                )
+            nc.sync.dma_start(out=rows_of(out, s, g0, g1), in_=result[s][:, g0:g1, :])
+
+        spread_q(0)
+        spread_k(0, 0, 0, PACK)
+        quant_q(0)
+        quant_k_half(0, 0)
+        spread_k(0, 1, 0, 2)
+        spread_k(0, 1, 2, 4)
+        quant_k_half(0, 1)
+        for g in range(SET):
+            scores(g)
+        spread_q(1)
+        scale_mask(0)
+        quant_q(1)
+        spread_v(0, 0)
+        cap(0)
+
+        side = {
+            0: ([(spread_v, 0, 1), (spread_q, 2)], [(quant_q, 2)]),
+            1: ([(scale_mask, 1)], [(quant_v, 0)]),
+            2: ([(spread_q, 3), (spread_k, 1, 0, 0, PACK)], [(quant_q, 3)]),
+            3: ([(scale_mask, 2)], [(spread_k, 1, 1, 0, PACK)]),
+            4: ([(spread_q, 4), (quant_k, 1, 0, N)], [(quant_q, 4)]),
+            5: ([(scale_mask, 3)], [(spread_v, 1, 0)]),
+            6: ([(spread_q, 5), (spread_v, 1, 1)], [(quant_q, 5)]),
+            7: ([(gate_y, 0)], [(finish, 0)]),
+            8: ([(spread_q, 6), (quant_v, 1)], [(quant_q, 6)]),
+            9: ([(gate_y, 1)], [(finish, 1)]),
+            10: ([(spread_q, 7), (gate_y, 2)], [(quant_q, 7), (finish, 2)]),
+            11: ([(gate_y, 3)], [(finish, 3)]),
+            12: ([(gate_y, 4)], [(finish, 4)]),
+            13: ([(gate_y, 5)], [(finish, 5)]),
+            14: ([(gate_y, 6)], [(finish, 6)]),
+        }
+        for m in range(PAIRS - 1):
+            cap(2 * m + 1)
+            cap(2 * m + 2)
+            if m >= 2 and m % 2 == 0:
+                gate_tanh(m // 2 - 1)
+            exponent(m, 0, 2)
+            if m == 2:
+                attend(0, 0, 2)
+            if m >= 2:
+                attend(m - 1, 0, 2)
+            weigh(m, 0, 2)
+            for job in side[m][0]:
+                job[0](*job[1:])
+            quant_w(m, 0, 2)
+            for job in side[m][1]:
+                job[0](*job[1:])
+
+        last, s = PAIRS - 1, STEPS - 1
+        cap(UNITS - 1)
+        exponent(last, 0, 1)
+        exponent(last, 1, 2)
+        gate_tanh(s)
+        attend(last - 1, 0, 2)
+        weigh(last, 0, 1)
+        weigh(last, 1, 2)
+        quant_w(last, 0, 1)
+        attend(last, 0, 1)
+        quant_w(last, 1, 2)
+        attend(last, 1, 2)
+        gate_y(s, 0, 2)
+        gate_y(s, 2, 3)
+        finish(s, 0, 2)
+        gate_y(s, 3, 4)
+        finish(s, 2, 3)
+        finish(s, 3, 4)

@@ -22,9 +22,8 @@ QT = 128
 TILES = NQ // QT
 STEPS = (H // SET) * TILES
 UNITS = STEPS * SET
-PAIRS = UNITS // 2
 W = QT * PACK
-HALF = N // 2
+K_SPLIT = 96
 
 
 def tile_rows_a_exp_mask_cap_gate_kernel(tc, qT, kT, t, v, mask, og, out):
@@ -61,28 +60,25 @@ def tile_rows_a_exp_mask_cap_gate_kernel(tc, qT, kT, t, v, mask, og, out):
             return load("og%d" % s, rows_of(og, s, 0, SET))
 
         q_raw, k_raw, v_raw, og_raw, m_raw = {}, {}, {}, {}, {}
-        q_raw[0] = load_features("q_raw0", qT, 0, 0, QT)[:]
-        k_raw[0, 0] = load_features("k_raw00", kT, 0, 0, HALF)[:]
-        k_raw[0, 1] = load_features("k_raw01", kT, 0, HALF, N)[:]
-        q_raw[1] = load_features("q_raw1", qT, 0, QT, 2 * QT)[:]
-        m_raw[0] = load_mask("m_raw0", 0, QT)[:]
+        k_raw[0] = load_features("k_raw0", kT, 0, 0, N)
+        q_raw[0, 0] = (load_features("q_raw0", qT, 0, 0, QT), 0)
+        m01 = load_mask("m_raw01", 0, 2 * QT)
         t_sb = load("t_sb", t.rearrange("(p j) o -> p (j o)", j=PACK))
+        q123 = load_features("q_raw123", qT, 0, QT, NQ)
+        for c in range(1, TILES):
+            q_raw[0, c] = (q123, 1)
         v_raw[0, 0] = load_values(0, 0)
         v_raw[0, 1] = load_values(0, 1)
-        q23 = load_features("q_raw23", qT, 0, 2 * QT, NQ)
-        q_raw[2], q_raw[3] = q23[:, :, 0:QT], q23[:, :, QT : 2 * QT]
-        m123 = load_mask("m_raw123", QT, NQ)
-        for c in range(1, TILES):
-            m_raw[c] = m123[:, :, QT * (c - 1) : QT * c]
+        m23 = load_mask("m_raw23", 2 * QT, NQ)
+        m_raw = [m01[:, :, 0:QT], m01[:, :, QT : 2 * QT], m23[:, :, 0:QT], m23[:, :, QT : 2 * QT]]
+        k_raw[1] = load_features("k_raw1", kT, 1, 0, N)
         og_raw[0] = load_gate(0)
-        k1 = load_features("k_raw1", kT, 1, 0, N)
-        k_raw[1, 0], k_raw[1, 1] = k1[:, :, 0:HALF], k1[:, :, HALF:N]
-        og_raw[1] = load_gate(1)
         q1 = load_features("q_raw4567", qT, 1, 0, NQ)
         for c in range(TILES):
-            q_raw[TILES + c] = q1[:, :, QT * c : QT * (c + 1)]
-        og_raw[2] = load_gate(2)
+            q_raw[1, c] = (q1, 0)
+        og_raw[1] = load_gate(1)
         v_raw[1, 0] = load_values(1, 0)
+        og_raw[2] = load_gate(2)
         v_raw[1, 1] = load_values(1, 1)
         for s in range(3, STEPS):
             og_raw[s] = load_gate(s)
@@ -93,13 +89,14 @@ def tile_rows_a_exp_mask_cap_gate_kernel(tc, qT, kT, t, v, mask, og, out):
         v_bf = [kept("v_bf%d" % a, [P, SET * W], BF16) for a in range(2)]
         v_codes = [kept("v_codes%d" % a, [P, SET * D], U32) for a in range(2)]
         v_scales = [kept("v_scales%d" % a, [P, SET * D], U8) for a in range(2)]
-        q_bf = [kept("q_bf%d" % s, [P, W], BF16) for s in range(STEPS)]
-        q_codes = [kept("q_codes%d" % s, [P, QT], U32) for s in range(STEPS)]
-        q_scales = [kept("q_scales%d" % s, [P, QT], U8) for s in range(STEPS)]
+        q_bf = [kept("q_bf%d" % a, [P, NQ * PACK], BF16) for a in range(2)]
+        q_codes = [kept("q_codes%d" % a, [P, NQ], U32) for a in range(2)]
+        q_scales = [kept("q_scales%d" % a, [P, NQ], U8) for a in range(2)]
         mask_t = [kept("mask_t%d" % c, [P, W], F32) for c in range(TILES)]
         gate = [kept("gate%d" % s, [P, SET, D], F32) for s in range(STEPS)]
         result = [kept("result%d" % s, [P, SET, D], F32) for s in range(STEPS)]
         recip = [kept("recip%d" % s, [P, SET], F32) for s in range(STEPS)]
+        half_recip = {s: kept("half_recip%d" % s, [P, SET], F32) for s in (STEPS - 1,)}
         score_bank = [psum.tile([P, W], F32, name="score_bank%d" % g) for g in range(SET)]
         y_bank = [psum.tile([P, SET, D], F32, name="y_bank%d" % b) for b in range(4)]
         capped, weights, w_bf, w_codes, w_scales = {}, {}, {}, {}, {}
@@ -107,28 +104,24 @@ def tile_rows_a_exp_mask_cap_gate_kernel(tc, qT, kT, t, v, mask, og, out):
         def quantize(codes, scales, values):
             nc.vector.quantize_mx(out=codes.bitcast(FP8X4), scales=scales, in_=values)
 
-        def spread_q(s):
+        def spread_q(a, c0, c1):
+            raw, first = q_raw[a, c0]
             nc.vector.tensor_copy(
-                out=q_bf[s][:].rearrange("p (c i j) -> p c j i", i=4, j=PACK),
-                in_=q_raw[s].rearrange("p j (c i) -> p c j i", i=4),
+                out=q_bf[a][:, W * c0 : W * c1].rearrange("p (c i j) -> p c j i", i=4, j=PACK),
+                in_=raw[:, :, QT * (c0 - first) : QT * (c1 - first)].rearrange("p j (c i) -> p c j i", i=4),
             )
 
-        def quant_q(s):
-            quantize(q_codes[s][:], q_scales[s][:], q_bf[s][:])
+        def quant_q(a, c0, c1):
+            quantize(q_codes[a][:, QT * c0 : QT * c1], q_scales[a][:, QT * c0 : QT * c1], q_bf[a][:, W * c0 : W * c1])
 
-        def spread_k(a, u, r0, r1):
-            s0, s1 = u * HALF // PACK, (u + 1) * HALF // PACK
-            nc.vector.tensor_copy(
+        def spread_k(a, s0, s1, r0, r1, copy=nc.vector.tensor_copy):
+            copy(
                 out=k_bf[a][:].rearrange("p (r s j) -> p s j r", r=PACK, j=PACK)[:, s0:s1, :, r0:r1],
-                in_=k_raw[a, u].rearrange("p j (s r) -> p s j r", r=PACK)[:, :, :, r0:r1],
+                in_=k_raw[a][:].rearrange("p j (s r) -> p s j r", r=PACK)[:, s0:s1, :, r0:r1],
             )
 
         def quant_k(a, c0, c1):
             quantize(k_codes[a][:, c0:c1], k_scales[a][:, c0:c1], k_bf[a][:, PACK * c0 : PACK * c1])
-
-        def quant_k_half(a, u):
-            for r in range(PACK):
-                quant_k(a, P * r + 64 * u, P * r + 64 * (u + 1))
 
         def spread_v(a, u):
             nc.vector.tensor_copy(
@@ -139,36 +132,42 @@ def tile_rows_a_exp_mask_cap_gate_kernel(tc, qT, kT, t, v, mask, og, out):
         def quant_v(a):
             quantize(v_codes[a][:], v_scales[a][:], v_bf[a][:])
 
-        def scale_mask(c):
-            nc.vector.tensor_tensor(
+        def scale_mask(rows):
+            for j in range(PACK):
+                nc.vector.tensor_scalar(out=rows[:, j, :], in0=rows[:, j, :], scalar1=t_sb[:, j : j + 1], scalar2=None, op0=ALU.mult)
+
+        def spread_mask(c):
+            nc.vector.tensor_copy(
                 out=mask_t[c][:].rearrange("p (q j) -> p q j", j=PACK),
-                in0=m_raw[c].rearrange("p j q -> p q j"),
-                in1=t_sb[:].unsqueeze(1).to_broadcast([P, QT, PACK]),
-                op=ALU.mult,
+                in_=m_raw[c].rearrange("p j q -> p q j"),
             )
 
         def scores(n):
             s, g = divmod(n, SET)
-            a = s // TILES
+            a, c = divmod(s, TILES)
             rows = slice(ROWS * g, ROWS * (g + 1))
+            queries = slice(QT * c, QT * (c + 1))
             for r in range(PACK):
                 cols = slice(P * r, P * (r + 1))
                 nc.tensor.matmul_mx(
                     out=score_bank[g][:, cols],
                     lhsT=k_codes[a][rows, cols].bitcast(FP8X4),
                     lhsT_scale=k_scales[a][rows, cols],
-                    rhs=q_codes[s][rows, :].bitcast(FP8X4),
-                    rhs_scale=q_scales[s][rows, :],
+                    rhs=q_codes[a][rows, queries].bitcast(FP8X4),
+                    rhs_scale=q_scales[a][rows, queries],
                     start=True,
                     stop=True,
                 )
 
+        groups = [(0, 1), (1, 2)] + [(n, n + 2) for n in range(2, UNITS - SET, 2)] + [(n, n + 1) for n in range(UNITS - SET, UNITS)]
+        group_of = {n: grp for grp in groups for n in range(*grp)}
+
         def cap(n):
-            m, i = divmod(n, 2)
-            if i == 0:
-                capped[m] = flow.tile([P, 2, W], F32, name="capped")
+            grp = group_of[n]
+            if n == grp[0]:
+                capped[grp] = flow.tile([P, grp[1] - grp[0], W], F32, name="capped")
             nc.scalar.activation(
-                out=capped[m][:, i, :].rearrange("p (q r) -> p q r", r=PACK),
+                out=capped[grp][:, n - grp[0], :].rearrange("p (q r) -> p q r", r=PACK),
                 in_=score_bank[n % SET][:].rearrange("p (r q) -> p q r", r=PACK),
                 func=ACT.Tanh,
                 scale=1.0 / CAP,
@@ -176,45 +175,43 @@ def tile_rows_a_exp_mask_cap_gate_kernel(tc, qT, kT, t, v, mask, og, out):
             if n + SET < UNITS:
                 scores(n + SET)
 
-        def exponent(m, i0, i1):
-            if i0 == 0:
-                weights[m] = flow.tile([P, 2, W], F32, name="weights", bufs=4)
-            nc.scalar.activation(out=weights[m][:, i0:i1, :], in_=capped[m][:, i0:i1, :], func=ACT.Exp, scale=CAP)
+        def exponent(grp):
+            weights[grp] = flow.tile([P, grp[1] - grp[0], W], F32, name="weights", bufs=5)
+            nc.scalar.activation(out=weights[grp][:], in_=capped[grp][:], func=ACT.Exp, scale=CAP)
 
         def gate_tanh(s):
             nc.scalar.activation(out=gate[s][:], in_=og_raw[s][:], func=ACT.Tanh, scale=0.5)
 
-        def weigh(m, i0, i1):
-            if i0 == 0:
-                w_bf[m] = flow.tile([P, 2 * W], BF16, name="w_bf", align_bytes=64)
-            c = (m // 2) % TILES
+        def weigh(grp):
+            width = grp[1] - grp[0]
+            w_bf[grp] = flow.tile([P, width, W], BF16, name="w_bf", align_bytes=64)
+            c = (grp[0] // SET) % TILES
             nc.vector.tensor_tensor(
-                out=w_bf[m][:, W * i0 : W * i1].rearrange("p (i x) -> p i x", x=W),
-                in0=weights[m][:, i0:i1, :],
-                in1=mask_t[c][:].unsqueeze(1).to_broadcast([P, i1 - i0, W]),
+                out=w_bf[grp][:],
+                in0=weights[grp][:],
+                in1=mask_t[c][:].unsqueeze(1).to_broadcast([P, width, W]),
                 op=ALU.mult,
             )
 
-        def quant_w(m, i0, i1):
-            if i0 == 0:
-                w_codes[m] = flow.tile([P, 2 * QT], U32, name="w_codes", align_bytes=64)
-                w_scales[m] = flow.tile([P, 2 * QT], U8, name="w_scales", align_bytes=64)
-            quantize(w_codes[m][:, QT * i0 : QT * i1], w_scales[m][:, QT * i0 : QT * i1], w_bf[m][:, W * i0 : W * i1])
+        def quant_w(grp):
+            width = grp[1] - grp[0]
+            w_codes[grp] = flow.tile([P, width * QT], U32, name="w_codes", align_bytes=64, bufs=5)
+            w_scales[grp] = flow.tile([P, width * QT], U8, name="w_scales", align_bytes=64, bufs=5)
+            quantize(w_codes[grp][:], w_scales[grp][:], w_bf[grp][:].rearrange("p i x -> p (i x)"))
 
         def y_of(n):
             s, g = divmod(n, SET)
-            bank = s % 4 if n < UNITS - 2 else n % 2
-            return y_bank[bank]
+            return y_bank[n % 2 if n >= UNITS - 2 else s % 4]
 
-        def attend(m, i0, i1):
-            for i in range(i0, i1):
-                n = 2 * m + i
+        def attend(grp):
+            for n in range(*grp):
                 s, g = divmod(n, SET)
                 a = s // TILES
+                cols = slice(QT * (n - grp[0]), QT * (n - grp[0] + 1))
                 nc.tensor.matmul_mx(
                     out=y_of(n)[:, g, :],
-                    lhsT=w_codes[m][:, QT * i : QT * (i + 1)].bitcast(FP8X4),
-                    lhsT_scale=w_scales[m][:, QT * i : QT * (i + 1)],
+                    lhsT=w_codes[grp][:, cols].bitcast(FP8X4),
+                    lhsT_scale=w_scales[grp][:, cols],
                     rhs=v_codes[a][:, D * g : D * (g + 1)].bitcast(FP8X4),
                     rhs_scale=v_scales[a][:, D * g : D * (g + 1)],
                     start=True,
@@ -245,70 +242,83 @@ def tile_rows_a_exp_mask_cap_gate_kernel(tc, qT, kT, t, v, mask, og, out):
                 )
             nc.sync.dma_start(out=rows_of(out, s, g0, g1), in_=result[s][:, g0:g1, :])
 
-        spread_q(0)
-        spread_k(0, 0, 0, PACK)
-        quant_q(0)
-        quant_k_half(0, 0)
-        spread_k(0, 1, 0, 2)
-        spread_k(0, 1, 2, 4)
-        quant_k_half(0, 1)
+        def finish_on_scalar(s, g0=0, g1=SET):
+            nc.scalar.mul(out=half_recip[s][:, g0:g1], in_=recip[s][:, g0:g1], mul=0.5)
+            for g in range(g0, g1):
+                nc.scalar.activation(out=result[s][:, g, :], in_=result[s][:, g, :], func=ACT.Copy, scale=half_recip[s][:, g : g + 1])
+            nc.sync.dma_start(out=rows_of(out, s, g0, g1), in_=result[s][:, g0:g1, :])
+
+        spread_k(0, 0, P, 0, 2)
+        spread_k(0, 0, K_SPLIT, 2, 4, nc.scalar.copy)
+        spread_k(0, K_SPLIT, P, 2, 4)
+        spread_q(0, 0, 1)
+        quant_k(0, 0, 2 * P)
+        quant_q(0, 0, 1)
+        quant_k(0, 2 * P, N)
         for g in range(SET):
             scores(g)
-        spread_q(1)
-        scale_mask(0)
-        quant_q(1)
-        spread_v(0, 0)
+        scale_mask(m01)
+        spread_mask(0)
+        spread_q(0, 1, 2)
+        spread_mask(1)
+        quant_q(0, 1, 2)
         cap(0)
 
         side = {
-            0: ([(spread_v, 0, 1), (spread_q, 2)], [(quant_q, 2)]),
-            1: ([(scale_mask, 1)], [(quant_v, 0)]),
-            2: ([(spread_q, 3), (spread_k, 1, 0, 0, PACK)], [(quant_q, 3)]),
-            3: ([(scale_mask, 2)], [(spread_k, 1, 1, 0, PACK)]),
-            4: ([(spread_q, 4), (quant_k, 1, 0, N)], [(quant_q, 4)]),
-            5: ([(scale_mask, 3)], [(spread_v, 1, 0)]),
-            6: ([(spread_q, 5), (spread_v, 1, 1)], [(quant_q, 5)]),
-            7: ([(gate_y, 0)], [(finish, 0)]),
-            8: ([(spread_q, 6), (quant_v, 1)], [(quant_q, 6)]),
-            9: ([(gate_y, 1)], [(finish, 1)]),
-            10: ([(spread_q, 7), (gate_y, 2)], [(quant_q, 7), (finish, 2)]),
-            11: ([(gate_y, 3)], [(finish, 3)]),
-            12: ([(gate_y, 4)], [(finish, 4)]),
-            13: ([(gate_y, 5)], [(finish, 5)]),
-            14: ([(gate_y, 6)], [(finish, 6)]),
+            0: ([(spread_q, 0, 2, 4)], [(quant_q, 0, 2, 4)]),
+            1: ([(spread_v, 0, 0)], [(spread_v, 0, 1)]),
+            2: ([(quant_v, 0)], [(scale_mask, m23)]),
+            4: ([(spread_mask, 2), (spread_mask, 3)], [(spread_k, 1, 0, 64, 0, PACK)]),
+            6: ([(spread_k, 1, 64, P, 0, PACK)], [(quant_k, 1, 0, N)]),
+            8: ([(spread_q, 1, 0, 2)], [(quant_q, 1, 0, 2)]),
+            10: ([(spread_q, 1, 2, 4)], [(quant_q, 1, 2, 4)]),
+            12: ([(spread_v, 1, 0)], [(spread_v, 1, 1)]),
+            14: ([(quant_v, 1), (gate_y, 0)], [(finish, 0)]),
+            16: ([(gate_y, 1)], [(finish, 1)]),
+            18: ([(gate_y, 2)], [(finish, 2)]),
+            20: ([(gate_y, 3)], [(finish, 3)]),
+            22: ([(gate_y, 4)], [(finish, 4)]),
+            24: ([(gate_y, 5)], []),
+            26: ([(finish, 5)], []),
+            28: ([(gate_y, 6)], []),
+            29: ([(finish, 6)], []),
         }
-        for m in range(PAIRS - 1):
-            cap(2 * m + 1)
-            cap(2 * m + 2)
-            if m >= 2 and m % 2 == 0:
-                gate_tanh(m // 2 - 1)
-            exponent(m, 0, 2)
-            if m == 2:
-                attend(0, 0, 2)
-            if m >= 2:
-                attend(m - 1, 0, 2)
-            weigh(m, 0, 2)
-            for job in side[m][0]:
+        gate_at = {10: 0, 12: 1, 14: 2, 16: 3, 20: 4, 22: 5, 28: 6}
+        capped_upto = 1
+        waiting = []
+        for grp in groups[:-2]:
+            for n in range(capped_upto, grp[1] + 1):
+                cap(n)
+            capped_upto = grp[1] + 1
+            if grp[0] in gate_at:
+                gate_tanh(gate_at[grp[0]])
+            exponent(grp)
+            if grp[0] > 4:
+                for old in waiting:
+                    attend(old)
+                waiting = []
+            weigh(grp)
+            for job in side[grp[0]][0]:
                 job[0](*job[1:])
-            quant_w(m, 0, 2)
-            for job in side[m][1]:
+            quant_w(grp)
+            waiting.append(grp)
+            for job in side[grp[0]][1]:
                 job[0](*job[1:])
 
-        last, s = PAIRS - 1, STEPS - 1
+        s = STEPS - 1
         cap(UNITS - 1)
-        exponent(last, 0, 1)
-        exponent(last, 1, 2)
+        exponent(groups[-2])
+        exponent(groups[-1])
         gate_tanh(s)
-        attend(last - 1, 0, 2)
-        weigh(last, 0, 1)
-        weigh(last, 1, 2)
-        quant_w(last, 0, 1)
-        attend(last, 0, 1)
-        quant_w(last, 1, 2)
-        attend(last, 1, 2)
+        attend(groups[-3])
+        weigh(groups[-2])
+        weigh(groups[-1])
+        quant_w(groups[-2])
+        attend(groups[-2])
+        quant_w(groups[-1])
+        attend(groups[-1])
         gate_y(s, 0, 2)
+        finish_on_scalar(s, 0, 2)
         gate_y(s, 2, 3)
-        finish(s, 0, 2)
         gate_y(s, 3, 4)
-        finish(s, 2, 3)
-        finish(s, 3, 4)
+        finish(s, 2, 4)

@@ -23,7 +23,7 @@ TILES = NQ // QT
 STEPS = (H // SET) * TILES
 UNITS = STEPS * SET
 W = QT * PACK
-K_SPLIT = 96
+HALF = N // 2
 
 
 def tile_rows_a_exp_mask_cap_gate_kernel(tc, qT, kT, t, v, mask, og, out):
@@ -60,19 +60,20 @@ def tile_rows_a_exp_mask_cap_gate_kernel(tc, qT, kT, t, v, mask, og, out):
             return load("og%d" % s, rows_of(og, s, 0, SET))
 
         q_raw, k_raw, v_raw, og_raw, m_raw = {}, {}, {}, {}, {}
-        k_raw[0] = load_features("k_raw0", kT, 0, 0, N)
+        k0 = load_features("k_raw0", kT, 0, 0, N)
+        k_raw[0, 0], k_raw[0, 1] = k0[:, :, 0:HALF], k0[:, :, HALF:N]
         q_raw[0, 0] = (load_features("q_raw0", qT, 0, 0, QT), 0)
+        og_raw[0] = load_gate(0)
+        q_raw[0, 1] = (load_features("q_raw1", qT, 0, QT, 2 * QT), 1)
         m01 = load_mask("m_raw01", 0, 2 * QT)
         t_sb = load("t_sb", t.rearrange("(p j) o -> p (j o)", j=PACK))
-        q123 = load_features("q_raw123", qT, 0, QT, NQ)
-        for c in range(1, TILES):
-            q_raw[0, c] = (q123, 1)
         v_raw[0, 0] = load_values(0, 0)
+        q_raw[0, 2] = (load_features("q_raw23", qT, 0, 2 * QT, NQ), 2)
         v_raw[0, 1] = load_values(0, 1)
         m23 = load_mask("m_raw23", 2 * QT, NQ)
         m_raw = [m01[:, :, 0:QT], m01[:, :, QT : 2 * QT], m23[:, :, 0:QT], m23[:, :, QT : 2 * QT]]
-        k_raw[1] = load_features("k_raw1", kT, 1, 0, N)
-        og_raw[0] = load_gate(0)
+        k1 = load_features("k_raw1", kT, 1, 0, N)
+        k_raw[1, 0], k_raw[1, 1] = k1[:, :, 0:HALF], k1[:, :, HALF:N]
         q1 = load_features("q_raw4567", qT, 1, 0, NQ)
         for c in range(TILES):
             q_raw[1, c] = (q1, 0)
@@ -96,7 +97,7 @@ def tile_rows_a_exp_mask_cap_gate_kernel(tc, qT, kT, t, v, mask, og, out):
         gate = [kept("gate%d" % s, [P, SET, D], F32) for s in range(STEPS)]
         result = [kept("result%d" % s, [P, SET, D], F32) for s in range(STEPS)]
         recip = [kept("recip%d" % s, [P, SET], F32) for s in range(STEPS)]
-        half_recip = {s: kept("half_recip%d" % s, [P, SET], F32) for s in (STEPS - 1,)}
+        half_recip = {s: kept("half_recip%d" % s, [P, SET], F32) for s in (STEPS - 2, STEPS - 1)}
         score_bank = [psum.tile([P, W], F32, name="score_bank%d" % g) for g in range(SET)]
         y_bank = [psum.tile([P, SET, D], F32, name="y_bank%d" % b) for b in range(4)]
         capped, weights, w_bf, w_codes, w_scales = {}, {}, {}, {}, {}
@@ -104,9 +105,9 @@ def tile_rows_a_exp_mask_cap_gate_kernel(tc, qT, kT, t, v, mask, og, out):
         def quantize(codes, scales, values):
             nc.vector.quantize_mx(out=codes.bitcast(FP8X4), scales=scales, in_=values)
 
-        def spread_q(a, c0, c1):
+        def spread_q(a, c0, c1, copy=nc.vector.tensor_copy):
             raw, first = q_raw[a, c0]
-            nc.vector.tensor_copy(
+            copy(
                 out=q_bf[a][:, W * c0 : W * c1].rearrange("p (c i j) -> p c j i", i=4, j=PACK),
                 in_=raw[:, :, QT * (c0 - first) : QT * (c1 - first)].rearrange("p j (c i) -> p c j i", i=4),
             )
@@ -114,14 +115,19 @@ def tile_rows_a_exp_mask_cap_gate_kernel(tc, qT, kT, t, v, mask, og, out):
         def quant_q(a, c0, c1):
             quantize(q_codes[a][:, QT * c0 : QT * c1], q_scales[a][:, QT * c0 : QT * c1], q_bf[a][:, W * c0 : W * c1])
 
-        def spread_k(a, s0, s1, r0, r1, copy=nc.vector.tensor_copy):
+        def spread_k(a, u, r0, r1, copy=nc.vector.tensor_copy):
+            s0, s1 = u * HALF // PACK, (u + 1) * HALF // PACK
             copy(
                 out=k_bf[a][:].rearrange("p (r s j) -> p s j r", r=PACK, j=PACK)[:, s0:s1, :, r0:r1],
-                in_=k_raw[a][:].rearrange("p j (s r) -> p s j r", r=PACK)[:, s0:s1, :, r0:r1],
+                in_=k_raw[a, u].rearrange("p j (s r) -> p s j r", r=PACK)[:, :, :, r0:r1],
             )
 
         def quant_k(a, c0, c1):
             quantize(k_codes[a][:, c0:c1], k_scales[a][:, c0:c1], k_bf[a][:, PACK * c0 : PACK * c1])
+
+        def quant_k_half(a, u, r0, r1):
+            for r in range(r0, r1):
+                quant_k(a, P * r + 64 * u, P * r + 64 * (u + 1))
 
         def spread_v(a, u):
             nc.vector.tensor_copy(
@@ -230,7 +236,7 @@ def tile_rows_a_exp_mask_cap_gate_kernel(tc, qT, kT, t, v, mask, og, out):
                 op1=ALU.mult,
             )
 
-        def finish(s, g0=0, g1=SET):
+        def finish(s, g0=0, g1=SET, queue=nc.sync):
             for g in range(g0, g1):
                 nc.vector.tensor_scalar(
                     out=result[s][:, g, :],
@@ -240,7 +246,7 @@ def tile_rows_a_exp_mask_cap_gate_kernel(tc, qT, kT, t, v, mask, og, out):
                     op0=ALU.mult,
                     op1=ALU.mult,
                 )
-            nc.sync.dma_start(out=rows_of(out, s, g0, g1), in_=result[s][:, g0:g1, :])
+            queue.dma_start(out=rows_of(out, s, g0, g1), in_=result[s][:, g0:g1, :])
 
         def finish_on_scalar(s, g0=0, g1=SET):
             nc.scalar.mul(out=half_recip[s][:, g0:g1], in_=recip[s][:, g0:g1], mul=0.5)
@@ -248,42 +254,45 @@ def tile_rows_a_exp_mask_cap_gate_kernel(tc, qT, kT, t, v, mask, og, out):
                 nc.scalar.activation(out=result[s][:, g, :], in_=result[s][:, g, :], func=ACT.Copy, scale=half_recip[s][:, g : g + 1])
             nc.sync.dma_start(out=rows_of(out, s, g0, g1), in_=result[s][:, g0:g1, :])
 
-        spread_k(0, 0, P, 0, 2)
-        spread_k(0, 0, K_SPLIT, 2, 4, nc.scalar.copy)
-        spread_k(0, K_SPLIT, P, 2, 4)
+        spread_k(0, 0, 0, 2)
+        spread_k(0, 1, 0, 2)
+        spread_k(0, 0, 2, 4, nc.scalar.copy)
+        spread_k(0, 1, 2, 4)
         spread_q(0, 0, 1)
         quant_k(0, 0, 2 * P)
         quant_q(0, 0, 1)
         quant_k(0, 2 * P, N)
+        gate_tanh(0)
         for g in range(SET):
             scores(g)
-        scale_mask(m01)
-        spread_mask(0)
         spread_q(0, 1, 2)
-        spread_mask(1)
+        scale_mask(m01)
         quant_q(0, 1, 2)
+        spread_mask(0)
+        spread_mask(1)
+        spread_v(0, 0)
         cap(0)
 
         side = {
             0: ([(spread_q, 0, 2, 4)], [(quant_q, 0, 2, 4)]),
-            1: ([(spread_v, 0, 0)], [(spread_v, 0, 1)]),
-            2: ([(quant_v, 0)], [(scale_mask, m23)]),
-            4: ([(spread_mask, 2), (spread_mask, 3)], [(spread_k, 1, 0, 64, 0, PACK)]),
-            6: ([(spread_k, 1, 64, P, 0, PACK)], [(quant_k, 1, 0, N)]),
-            8: ([(spread_q, 1, 0, 2)], [(quant_q, 1, 0, 2)]),
-            10: ([(spread_q, 1, 2, 4)], [(quant_q, 1, 2, 4)]),
-            12: ([(spread_v, 1, 0)], [(spread_v, 1, 1)]),
-            14: ([(quant_v, 1), (gate_y, 0)], [(finish, 0)]),
-            16: ([(gate_y, 1)], [(finish, 1)]),
-            18: ([(gate_y, 2)], [(finish, 2)]),
-            20: ([(gate_y, 3)], [(finish, 3)]),
-            22: ([(gate_y, 4)], [(finish, 4)]),
+            1: ([(spread_v, 0, 1)], [(quant_v, 0)]),
+            2: ([(scale_mask, m23)], [(spread_mask, 2), (spread_mask, 3)]),
+            4: ([(spread_k, 1, 0, 0, PACK)], [(spread_k, 1, 1, 0, PACK)]),
+            6: ([(quant_k, 1, 0, N)], [(spread_q, 1, 0, 2)]),
+            8: ([(quant_q, 1, 0, 2), (spread_q, 1, 2, 4)], [(quant_q, 1, 2, 4)]),
+            10: ([(spread_v, 1, 0)], [(spread_v, 1, 1)]),
+            12: ([(gate_y, 0)], [(finish, 0)]),
+            14: ([(quant_v, 1), (gate_y, 1)], [(finish, 1)]),
+            16: ([(gate_y, 2)], [(finish, 2)]),
+            18: ([(gate_y, 3)], [(finish, 3)]),
+            20: ([(gate_y, 4)], []),
+            22: ([(finish, 4)], []),
             24: ([(gate_y, 5)], []),
             26: ([(finish, 5)], []),
             28: ([(gate_y, 6)], []),
-            29: ([(finish, 6)], []),
+            29: ([], []),
         }
-        gate_at = {10: 0, 12: 1, 14: 2, 16: 3, 20: 4, 22: 5, 28: 6}
+        gate_at = {10: 1, 12: 2, 14: 3, 16: 4, 20: 5, 28: 6}
         capped_upto = 1
         waiting = []
         for grp in groups[:-2]:
@@ -293,7 +302,7 @@ def tile_rows_a_exp_mask_cap_gate_kernel(tc, qT, kT, t, v, mask, og, out):
             if grp[0] in gate_at:
                 gate_tanh(gate_at[grp[0]])
             exponent(grp)
-            if grp[0] > 4:
+            if grp[0] > 1:
                 for old in waiting:
                     attend(old)
                 waiting = []
@@ -310,6 +319,7 @@ def tile_rows_a_exp_mask_cap_gate_kernel(tc, qT, kT, t, v, mask, og, out):
         exponent(groups[-2])
         exponent(groups[-1])
         gate_tanh(s)
+        finish_on_scalar(s - 1)
         attend(groups[-3])
         weigh(groups[-2])
         weigh(groups[-1])
@@ -321,4 +331,5 @@ def tile_rows_a_exp_mask_cap_gate_kernel(tc, qT, kT, t, v, mask, og, out):
         finish_on_scalar(s, 0, 2)
         gate_y(s, 2, 3)
         gate_y(s, 3, 4)
-        finish(s, 2, 4)
+        finish(s, 2, 3)
+        finish(s, 3, 4, nc.scalar)

@@ -18,12 +18,18 @@ P = 128
 PACK = 4
 ROWS = D // PACK
 SET = P // ROWS
+SETS = H // SET
 QT = 128
 TILES = NQ // QT
-STEPS = (H // SET) * TILES
+STEPS = SETS * TILES
 UNITS = STEPS * SET
 W = QT * PACK
 HALF = N // 2
+RUN = 4
+Y_BANKS = 4
+PENDING = 5
+FIRST_GATED = 12
+GATE_LEAD = 4
 
 
 def tile_rows_a_exp_mask_cap_gate_kernel(tc, qT, kT, t, v, mask, og, out):
@@ -59,7 +65,7 @@ def tile_rows_a_exp_mask_cap_gate_kernel(tc, qT, kT, t, v, mask, og, out):
         def load_gate(s):
             return load("og%d" % s, rows_of(og, s, 0, SET))
 
-        q_raw, k_raw, v_raw, og_raw, m_raw = {}, {}, {}, {}, {}
+        q_raw, k_raw, v_raw, og_raw = {}, {}, {}, {}
         k0 = load_features("k_raw0", kT, 0, 0, N)
         k_raw[0, 0], k_raw[0, 1] = k0[:, :, 0:HALF], k0[:, :, HALF:N]
         q_raw[0, 0] = (load_features("q_raw0", qT, 0, 0, QT), 0)
@@ -75,8 +81,7 @@ def tile_rows_a_exp_mask_cap_gate_kernel(tc, qT, kT, t, v, mask, og, out):
         k1 = load_features("k_raw1", kT, 1, 0, N)
         k_raw[1, 0], k_raw[1, 1] = k1[:, :, 0:HALF], k1[:, :, HALF:N]
         q1 = load_features("q_raw4567", qT, 1, 0, NQ)
-        for c in range(TILES):
-            q_raw[1, c] = (q1, 0)
+        q_raw[1, 0], q_raw[1, 2] = (q1, 0), (q1, 0)
         og_raw[1] = load_gate(1)
         v_raw[1, 0] = load_values(1, 0)
         og_raw[2] = load_gate(2)
@@ -84,55 +89,52 @@ def tile_rows_a_exp_mask_cap_gate_kernel(tc, qT, kT, t, v, mask, og, out):
         for s in range(3, STEPS):
             og_raw[s] = load_gate(s)
 
-        k_bf = [kept("k_bf%d" % a, [P, N * PACK], BF16) for a in range(2)]
-        k_codes = [kept("k_codes%d" % a, [P, N], U32) for a in range(2)]
-        k_scales = [kept("k_scales%d" % a, [P, N], U8) for a in range(2)]
-        v_bf = [kept("v_bf%d" % a, [P, SET * W], BF16) for a in range(2)]
-        v_codes = [kept("v_codes%d" % a, [P, SET * D], U32) for a in range(2)]
-        v_scales = [kept("v_scales%d" % a, [P, SET * D], U8) for a in range(2)]
-        q_bf = [kept("q_bf%d" % a, [P, NQ * PACK], BF16) for a in range(2)]
-        q_codes = [kept("q_codes%d" % a, [P, NQ], U32) for a in range(2)]
-        q_scales = [kept("q_scales%d" % a, [P, NQ], U8) for a in range(2)]
+        k_bf = [kept("k_bf%d" % a, [P, N * PACK], BF16) for a in range(SETS)]
+        k_codes = [kept("k_codes%d" % a, [P, N], U32) for a in range(SETS)]
+        k_scales = [kept("k_scales%d" % a, [P, N], U8) for a in range(SETS)]
+        v_bf = [kept("v_bf%d" % a, [P, SET * D * PACK], BF16) for a in range(SETS)]
+        v_codes = [kept("v_codes%d" % a, [P, SET * D], U32) for a in range(SETS)]
+        v_scales = [kept("v_scales%d" % a, [P, SET * D], U8) for a in range(SETS)]
+        q_bf = [kept("q_bf%d" % a, [P, NQ * PACK], BF16) for a in range(SETS)]
+        q_codes = [kept("q_codes%d" % a, [P, NQ], U32) for a in range(SETS)]
+        q_scales = [kept("q_scales%d" % a, [P, NQ], U8) for a in range(SETS)]
         mask_t = [kept("mask_t%d" % c, [P, W], F32) for c in range(TILES)]
         gate = [kept("gate%d" % s, [P, SET, D], F32) for s in range(STEPS)]
         result = [kept("result%d" % s, [P, SET, D], F32) for s in range(STEPS)]
         recip = [kept("recip%d" % s, [P, SET], F32) for s in range(STEPS)]
         half_recip = {s: kept("half_recip%d" % s, [P, SET], F32) for s in (STEPS - 2, STEPS - 1)}
         score_bank = [psum.tile([P, W], F32, name="score_bank%d" % g) for g in range(SET)]
-        y_bank = [psum.tile([P, SET, D], F32, name="y_bank%d" % b) for b in range(4)]
+        y_bank = [psum.tile([P, SET, D], F32, name="y_bank%d" % b) for b in range(Y_BANKS)]
         capped, weights, w_bf, w_codes, w_scales = {}, {}, {}, {}, {}
 
         def quantize(codes, scales, values):
             nc.vector.quantize_mx(out=codes.bitcast(FP8X4), scales=scales, in_=values)
 
-        def spread_q(a, c0, c1, copy=nc.vector.tensor_copy):
+        def spread_q(a, c0, c1):
             raw, first = q_raw[a, c0]
-            copy(
-                out=q_bf[a][:, W * c0 : W * c1].rearrange("p (c i j) -> p c j i", i=4, j=PACK),
-                in_=raw[:, :, QT * (c0 - first) : QT * (c1 - first)].rearrange("p j (c i) -> p c j i", i=4),
+            nc.vector.tensor_copy(
+                out=q_bf[a][:, W * c0 : W * c1].rearrange("p (c i j) -> p c j i", i=RUN, j=PACK),
+                in_=raw[:, :, QT * (c0 - first) : QT * (c1 - first)].rearrange("p j (c i) -> p c j i", i=RUN),
             )
 
         def quant_q(a, c0, c1):
             quantize(q_codes[a][:, QT * c0 : QT * c1], q_scales[a][:, QT * c0 : QT * c1], q_bf[a][:, W * c0 : W * c1])
 
         def spread_k(a, u, r0, r1, copy=nc.vector.tensor_copy):
-            s0, s1 = u * HALF // PACK, (u + 1) * HALF // PACK
+            x0, x1 = u * HALF // PACK, (u + 1) * HALF // PACK
             copy(
-                out=k_bf[a][:].rearrange("p (r s j) -> p s j r", r=PACK, j=PACK)[:, s0:s1, :, r0:r1],
-                in_=k_raw[a, u].rearrange("p j (s r) -> p s j r", r=PACK)[:, :, :, r0:r1],
+                out=k_bf[a][:].rearrange("p (r x j) -> p x j r", r=PACK, j=PACK)[:, x0:x1, :, r0:r1],
+                in_=k_raw[a, u].rearrange("p j (x r) -> p x j r", r=PACK)[:, :, :, r0:r1],
             )
 
         def quant_k(a, c0, c1):
             quantize(k_codes[a][:, c0:c1], k_scales[a][:, c0:c1], k_bf[a][:, PACK * c0 : PACK * c1])
 
-        def quant_k_half(a, u, r0, r1):
-            for r in range(r0, r1):
-                quant_k(a, P * r + 64 * u, P * r + 64 * (u + 1))
-
         def spread_v(a, u):
+            width = 2 * D * PACK
             nc.vector.tensor_copy(
-                out=v_bf[a][:, 2 * W * u : 2 * W * (u + 1)].rearrange("p (h c i j) -> p h c j i", h=2, i=4, j=PACK),
-                in_=v_raw[a, u][:].rearrange("p h (j c i) -> p h c j i", j=PACK, i=4),
+                out=v_bf[a][:, width * u : width * (u + 1)].rearrange("p (h c i j) -> p h c j i", h=2, i=RUN, j=PACK),
+                in_=v_raw[a, u][:].rearrange("p h (j c i) -> p h c j i", j=PACK, i=RUN),
             )
 
         def quant_v(a):
@@ -148,24 +150,27 @@ def tile_rows_a_exp_mask_cap_gate_kernel(tc, qT, kT, t, v, mask, og, out):
                 in_=m_raw[c].rearrange("p j q -> p q j"),
             )
 
-        def scores(n):
-            s, g = divmod(n, SET)
-            a, c = divmod(s, TILES)
-            rows = slice(ROWS * g, ROWS * (g + 1))
-            queries = slice(QT * c, QT * (c + 1))
+        def scores(units):
             for r in range(PACK):
                 cols = slice(P * r, P * (r + 1))
-                nc.tensor.matmul_mx(
-                    out=score_bank[g][:, cols],
-                    lhsT=k_codes[a][rows, cols].bitcast(FP8X4),
-                    lhsT_scale=k_scales[a][rows, cols],
-                    rhs=q_codes[a][rows, queries].bitcast(FP8X4),
-                    rhs_scale=q_scales[a][rows, queries],
-                    start=True,
-                    stop=True,
-                )
+                for n in units:
+                    s, g = divmod(n, SET)
+                    a, c = divmod(s, TILES)
+                    rows = slice(ROWS * g, ROWS * (g + 1))
+                    queries = slice(QT * c, QT * (c + 1))
+                    nc.tensor.matmul_mx(
+                        out=score_bank[g][:, cols],
+                        lhsT=k_codes[a][rows, cols].bitcast(FP8X4),
+                        lhsT_scale=k_scales[a][rows, cols],
+                        rhs=q_codes[a][rows, queries].bitcast(FP8X4),
+                        rhs_scale=q_scales[a][rows, queries],
+                        start=True,
+                        stop=True,
+                    )
 
-        groups = [(0, 1), (1, 2)] + [(n, n + 2) for n in range(2, UNITS - SET, 2)] + [(n, n + 1) for n in range(UNITS - SET, UNITS)]
+        groups = [(0, 1), (1, 2)]
+        groups.extend((n, n + 2) for n in range(2, UNITS - SET, 2))
+        groups.extend((n, n + 1) for n in range(UNITS - SET, UNITS))
         group_of = {n: grp for grp in groups for n in range(*grp)}
 
         def cap(n):
@@ -178,11 +183,11 @@ def tile_rows_a_exp_mask_cap_gate_kernel(tc, qT, kT, t, v, mask, og, out):
                 func=ACT.Tanh,
                 scale=1.0 / CAP,
             )
-            if n + SET < UNITS:
-                scores(n + SET)
+            if n % 2 == 0 and n <= UNITS - SET:
+                scores([m + SET for m in (n - 1, n) if 0 <= m < UNITS - SET])
 
         def exponent(grp):
-            weights[grp] = flow.tile([P, grp[1] - grp[0], W], F32, name="weights", bufs=5)
+            weights[grp] = flow.tile([P, grp[1] - grp[0], W], F32, name="weights", bufs=PENDING)
             nc.scalar.activation(out=weights[grp][:], in_=capped[grp][:], func=ACT.Exp, scale=CAP)
 
         def gate_tanh(s):
@@ -201,13 +206,12 @@ def tile_rows_a_exp_mask_cap_gate_kernel(tc, qT, kT, t, v, mask, og, out):
 
         def quant_w(grp):
             width = grp[1] - grp[0]
-            w_codes[grp] = flow.tile([P, width * QT], U32, name="w_codes", align_bytes=64, bufs=5)
-            w_scales[grp] = flow.tile([P, width * QT], U8, name="w_scales", align_bytes=64, bufs=5)
+            w_codes[grp] = flow.tile([P, width * QT], U32, name="w_codes", align_bytes=64, bufs=PENDING)
+            w_scales[grp] = flow.tile([P, width * QT], U8, name="w_scales", align_bytes=64, bufs=PENDING)
             quantize(w_codes[grp][:], w_scales[grp][:], w_bf[grp][:].rearrange("p i x -> p (i x)"))
 
         def y_of(n):
-            s, g = divmod(n, SET)
-            return y_bank[n % 2 if n >= UNITS - 2 else s % 4]
+            return y_bank[n % 2 if n >= UNITS - 2 else (n // SET) % Y_BANKS]
 
         def attend(grp):
             for n in range(*grp):
@@ -256,43 +260,50 @@ def tile_rows_a_exp_mask_cap_gate_kernel(tc, qT, kT, t, v, mask, og, out):
 
         spread_k(0, 0, 0, 2)
         spread_k(0, 1, 0, 2)
-        spread_k(0, 0, 2, 4, nc.scalar.copy)
-        spread_k(0, 1, 2, 4)
+        spread_k(0, 0, 2, PACK, nc.scalar.copy)
+        spread_k(0, 1, 2, PACK)
         spread_q(0, 0, 1)
-        quant_k(0, 0, 2 * P)
+        quant_k(0, 0, HALF)
         quant_q(0, 0, 1)
-        quant_k(0, 2 * P, N)
+        quant_k(0, HALF, N)
         gate_tanh(0)
-        for g in range(SET):
-            scores(g)
+        scores([0, 1])
+        scores([2, 3])
         spread_q(0, 1, 2)
-        scale_mask(m01)
         quant_q(0, 1, 2)
+        scale_mask(m01)
         spread_mask(0)
         spread_mask(1)
         spread_v(0, 0)
         cap(0)
 
-        side = {
-            0: ([(spread_q, 0, 2, 4)], [(quant_q, 0, 2, 4)]),
-            1: ([(spread_v, 0, 1)], [(quant_v, 0)]),
-            2: ([(scale_mask, m23)], [(spread_mask, 2), (spread_mask, 3)]),
-            4: ([(spread_k, 1, 0, 0, PACK)], [(spread_k, 1, 1, 0, PACK)]),
-            6: ([(quant_k, 1, 0, N)], [(spread_q, 1, 0, 2)]),
-            8: ([(quant_q, 1, 0, 2), (spread_q, 1, 2, 4)], [(quant_q, 1, 2, 4)]),
-            10: ([(spread_v, 1, 0)], [(spread_v, 1, 1)]),
-            12: ([(gate_y, 0)], [(finish, 0)]),
-            14: ([(quant_v, 1), (gate_y, 1)], [(finish, 1)]),
-            16: ([(gate_y, 2)], [(finish, 2)]),
-            18: ([(gate_y, 3)], [(finish, 3)]),
-            20: ([(gate_y, 4)], []),
-            22: ([(finish, 4)], []),
-            24: ([(gate_y, 5)], []),
-            26: ([(finish, 5)], []),
-            28: ([(gate_y, 6)], []),
-            29: ([], []),
-        }
-        gate_at = {10: 1, 12: 2, 14: 3, 16: 4, 20: 5, 28: 6}
+        before = {grp[0]: [] for grp in groups}
+        after = {grp[0]: [] for grp in groups}
+        operands = [
+            ([(spread_q, 0, 2, TILES)], [(quant_q, 0, 2, TILES)]),
+            ([(spread_v, 0, 1)], [(quant_v, 0)]),
+            ([(scale_mask, m23)], [(spread_mask, 2), (spread_mask, 3)]),
+            ([(spread_k, 1, 0, 0, PACK)], [(spread_k, 1, 1, 0, PACK)]),
+            ([(quant_k, 1, 0, N)], [(spread_q, 1, 0, 2)]),
+            ([(quant_q, 1, 0, 2), (spread_q, 1, 2, TILES)], [(quant_q, 1, 2, TILES)]),
+            ([(spread_v, 1, 0)], [(spread_v, 1, 1)]),
+        ]
+        for grp, (jobs_before, jobs_after) in zip(groups, operands):
+            before[grp[0]].extend(jobs_before)
+            after[grp[0]].extend(jobs_after)
+        before[FIRST_GATED + 2].append((quant_v, 1))
+        last = STEPS - 1
+        gate_at = {}
+        for s in range(last):
+            n = max(FIRST_GATED + 2 * s, SET * (s + 1))
+            before[n].append((gate_y, s))
+            if n > SET * (s + 1):
+                after[n].append((finish, s))
+            elif s < last - 1:
+                before[n + 2].append((finish, s))
+            if s > 0:
+                gate_at[n - GATE_LEAD if s < last - 1 else n] = s
+
         capped_upto = 1
         waiting = []
         for grp in groups[:-2]:
@@ -302,34 +313,33 @@ def tile_rows_a_exp_mask_cap_gate_kernel(tc, qT, kT, t, v, mask, og, out):
             if grp[0] in gate_at:
                 gate_tanh(gate_at[grp[0]])
             exponent(grp)
-            if grp[0] > 1:
-                for old in waiting:
-                    attend(old)
+            if grp[0] % SET == 0:
+                for done in waiting:
+                    attend(done)
                 waiting = []
             weigh(grp)
-            for job in side[grp[0]][0]:
+            for job in before[grp[0]]:
                 job[0](*job[1:])
             quant_w(grp)
             waiting.append(grp)
-            for job in side[grp[0]][1]:
+            for job in after[grp[0]]:
                 job[0](*job[1:])
 
-        s = STEPS - 1
         cap(UNITS - 1)
         exponent(groups[-2])
         exponent(groups[-1])
-        gate_tanh(s)
-        finish_on_scalar(s - 1)
-        attend(groups[-3])
+        gate_tanh(last)
+        finish_on_scalar(last - 1)
+        for done in waiting:
+            attend(done)
         weigh(groups[-2])
         weigh(groups[-1])
-        quant_w(groups[-2])
-        attend(groups[-2])
-        quant_w(groups[-1])
-        attend(groups[-1])
-        gate_y(s, 0, 2)
-        finish_on_scalar(s, 0, 2)
-        gate_y(s, 2, 3)
-        gate_y(s, 3, 4)
-        finish(s, 2, 3)
-        finish(s, 3, 4, nc.scalar)
+        for grp in groups[-2:]:
+            quant_w(grp)
+            attend(grp)
+        gate_y(last, 0, 2)
+        finish_on_scalar(last, 0, 2)
+        gate_y(last, 2, 3)
+        gate_y(last, 3, SET)
+        finish(last, 2, 3)
+        finish(last, 3, SET, nc.scalar)

from contextlib import ExitStack

import concourse.mybir as mybir

H, D, NQ, N = 8, 128, 512, 512
CAP = 2.0
FLOPS = 2 * 2 * H * NQ * N * D

F32 = mybir.dt.float32
BF16 = mybir.dt.bfloat16
U32 = mybir.dt.uint32
U8 = mybir.dt.uint8
FP8X4 = mybir.dt.float8_e4m3fn_x4
ACT = mybir.ActivationFunctionType
ALU = mybir.AluOpType

P = 128
PACK = 4
ROWS = D // PACK
SET = P // ROWS
SETS = H // SET
QT = 128
TILES = NQ // QT
STEPS = SETS * TILES
UNITS = STEPS * SET
W = QT * PACK
HALF = N // 2
RUN = 4
Y_BANKS = 4
PENDING = 5
FIRST_GATED = 12
GATE_LEAD = 4


def tile_rows_a_exp_mask_cap_gate_kernel(tc, qT, kT, t, v, mask, og, out):
    nc = tc.nc
    with ExitStack() as ctx:
        keep = ctx.enter_context(tc.tile_pool(name="keep", bufs=1))
        flow = ctx.enter_context(tc.tile_pool(name="flow", bufs=3))
        psum = ctx.enter_context(tc.psum_pool(name="psum", bufs=1))
        ctx.enter_context(tc.manual_schedule())

        def kept(name, shape, dtype):
            return keep.tile(shape, dtype, name=name, align_bytes=64)

        def load(name, src):
            dst = kept(name, list(src.shape), F32)
            nc.sync.dma_start(out=dst[:], in_=src)
            return dst

        def load_features(name, x, a, c0, c1):
            return load(name, x[SET * a : SET * (a + 1), :, c0:c1].rearrange("h (p j) n -> (h p) j n", j=PACK))

        def load_mask(name, c0, c1):
            return load(name, mask[:, c0:c1].rearrange("(p j) q -> p j q", j=PACK))

        def load_values(a, u):
            h0 = SET * a + 2 * u
            return load("v_raw%d_%d" % (a, u), v[h0 : h0 + 2].rearrange("h (p j) e -> p h (j e)", j=PACK))

        def rows_of(x, s, g0, g1):
            a, c = divmod(s, TILES)
            return x[SET * a + g0 : SET * a + g1, QT * c : QT * (c + 1), :].rearrange("h q e -> q h e")

        def load_gate(s):
            return load("og%d" % s, rows_of(og, s, 0, SET))

        q_raw, k_raw, v_raw, og_raw = {}, {}, {}, {}
        k0 = load_features("k_raw0", kT, 0, 0, N)
        k_raw[0, 0], k_raw[0, 1] = k0[:, :, 0:HALF], k0[:, :, HALF:N]
        q_raw[0, 0] = (load_features("q_raw0", qT, 0, 0, QT), 0)
        og_raw[0] = load_gate(0)
        q_raw[0, 1] = (load_features("q_raw1", qT, 0, QT, 2 * QT), 1)
        m01 = load_mask("m_raw01", 0, 2 * QT)
        t_sb = load("t_sb", t.rearrange("(p j) o -> p (j o)", j=PACK))
        v_raw[0, 0] = load_values(0, 0)
        q_raw[0, 2] = (load_features("q_raw23", qT, 0, 2 * QT, NQ), 2)
        v_raw[0, 1] = load_values(0, 1)
        m23 = load_mask("m_raw23", 2 * QT, NQ)
        m_raw = [m01[:, :, 0:QT], m01[:, :, QT : 2 * QT], m23[:, :, 0:QT], m23[:, :, QT : 2 * QT]]
        k1 = load_features("k_raw1", kT, 1, 0, N)
        k_raw[1, 0], k_raw[1, 1] = k1[:, :, 0:HALF], k1[:, :, HALF:N]
        q1 = load_features("q_raw4567", qT, 1, 0, NQ)
        q_raw[1, 0], q_raw[1, 2] = (q1, 0), (q1, 0)
        og_raw[1] = load_gate(1)
        v_raw[1, 0] = load_values(1, 0)
        og_raw[2] = load_gate(2)
        v_raw[1, 1] = load_values(1, 1)
        for s in range(3, STEPS):
            og_raw[s] = load_gate(s)

        k_bf = [kept("k_bf%d" % a, [P, N * PACK], BF16) for a in range(SETS)]
        k_codes = [kept("k_codes%d" % a, [P, N], U32) for a in range(SETS)]
        k_scales = [kept("k_scales%d" % a, [P, N], U8) for a in range(SETS)]
        v_bf = [kept("v_bf%d" % a, [P, SET * D * PACK], BF16) for a in range(SETS)]
        v_codes = [kept("v_codes%d" % a, [P, SET * D], U32) for a in range(SETS)]
        v_scales = [kept("v_scales%d" % a, [P, SET * D], U8) for a in range(SETS)]
        q_bf = [kept("q_bf%d" % a, [P, NQ * PACK], BF16) for a in range(SETS)]
        q_codes = [kept("q_codes%d" % a, [P, NQ], U32) for a in range(SETS)]
        q_scales = [kept("q_scales%d" % a, [P, NQ], U8) for a in range(SETS)]
        mask_t = [kept("mask_t%d" % c, [P, W], F32) for c in range(TILES)]
        gate = [kept("gate%d" % s, [P, SET, D], F32) for s in range(STEPS)]
        result = [kept("result%d" % s, [P, SET, D], F32) for s in range(STEPS)]
        recip = [kept("recip%d" % s, [P, SET], F32) for s in range(STEPS)]
        half_recip = {s: kept("half_recip%d" % s, [P, SET], F32) for s in (STEPS - 2, STEPS - 1)}
        score_bank = [psum.tile([P, W], F32, name="score_bank%d" % g) for g in range(SET)]
        y_bank = [psum.tile([P, SET, D], F32, name="y_bank%d" % b) for b in range(Y_BANKS)]
        capped, weights, w_bf, w_codes, w_scales = {}, {}, {}, {}, {}

        def quantize(codes, scales, values):
            nc.vector.quantize_mx(out=codes.bitcast(FP8X4), scales=scales, in_=values)

        def spread_q(a, c0, c1):
            raw, first = q_raw[a, c0]
            nc.vector.tensor_copy(
                out=q_bf[a][:, W * c0 : W * c1].rearrange("p (c i j) -> p c j i", i=RUN, j=PACK),
                in_=raw[:, :, QT * (c0 - first) : QT * (c1 - first)].rearrange("p j (c i) -> p c j i", i=RUN),
            )

        def quant_q(a, c0, c1):
            quantize(q_codes[a][:, QT * c0 : QT * c1], q_scales[a][:, QT * c0 : QT * c1], q_bf[a][:, W * c0 : W * c1])

        def spread_k(a, u, r0, r1, copy=nc.vector.tensor_copy):
            x0, x1 = u * HALF // PACK, (u + 1) * HALF // PACK
            copy(
                out=k_bf[a][:].rearrange("p (r x j) -> p x j r", r=PACK, j=PACK)[:, x0:x1, :, r0:r1],
                in_=k_raw[a, u].rearrange("p j (x r) -> p x j r", r=PACK)[:, :, :, r0:r1],
            )

        def quant_k(a, c0, c1):
            quantize(k_codes[a][:, c0:c1], k_scales[a][:, c0:c1], k_bf[a][:, PACK * c0 : PACK * c1])

        def spread_v(a, u):
            width = 2 * D * PACK
            nc.vector.tensor_copy(
                out=v_bf[a][:, width * u : width * (u + 1)].rearrange("p (h c i j) -> p h c j i", h=2, i=RUN, j=PACK),
                in_=v_raw[a, u][:].rearrange("p h (j c i) -> p h c j i", j=PACK, i=RUN),
            )

        def quant_v(a):
            quantize(v_codes[a][:], v_scales[a][:], v_bf[a][:])

        def scale_mask(rows):
            for j in range(PACK):
                nc.vector.tensor_scalar(out=rows[:, j, :], in0=rows[:, j, :], scalar1=t_sb[:, j : j + 1], scalar2=None, op0=ALU.mult)

        def spread_mask(c):
            nc.vector.tensor_copy(
                out=mask_t[c][:].rearrange("p (q j) -> p q j", j=PACK),
                in_=m_raw[c].rearrange("p j q -> p q j"),
            )

        def scores(units):
            for r in range(PACK):
                cols = slice(P * r, P * (r + 1))
                for n in units:
                    s, g = divmod(n, SET)
                    a, c = divmod(s, TILES)
                    rows = slice(ROWS * g, ROWS * (g + 1))
                    queries = slice(QT * c, QT * (c + 1))
                    nc.tensor.matmul_mx(
                        out=score_bank[g][:, cols],
                        lhsT=k_codes[a][rows, cols].bitcast(FP8X4),
                        lhsT_scale=k_scales[a][rows, cols],
                        rhs=q_codes[a][rows, queries].bitcast(FP8X4),
                        rhs_scale=q_scales[a][rows, queries],
                        start=True,
                        stop=True,
                    )

        groups = [(0, 1), (1, 2)]
        groups.extend((n, n + 2) for n in range(2, UNITS - SET, 2))
        groups.extend((n, n + 1) for n in range(UNITS - SET, UNITS))
        group_of = {n: grp for grp in groups for n in range(*grp)}

        def cap(n):
            grp = group_of[n]
            if n == grp[0]:
                capped[grp] = flow.tile([P, grp[1] - grp[0], W], F32, name="capped")
            nc.scalar.activation(
                out=capped[grp][:, n - grp[0], :].rearrange("p (q r) -> p q r", r=PACK),
                in_=score_bank[n % SET][:].rearrange("p (r q) -> p q r", r=PACK),
                func=ACT.Tanh,
                scale=1.0 / CAP,
            )
            if n % 2 == 0 and n <= UNITS - SET:
                scores([m + SET for m in (n - 1, n) if 0 <= m < UNITS - SET])

        def exponent(grp):
            weights[grp] = flow.tile([P, grp[1] - grp[0], W], F32, name="weights", bufs=PENDING)
            nc.scalar.activation(out=weights[grp][:], in_=capped[grp][:], func=ACT.Exp, scale=CAP)

        def gate_tanh(s):
            nc.scalar.activation(out=gate[s][:], in_=og_raw[s][:], func=ACT.Tanh, scale=0.5)

        def weigh(grp):
            width = grp[1] - grp[0]
            w_bf[grp] = flow.tile([P, width, W], BF16, name="w_bf", align_bytes=64)
            c = (grp[0] // SET) % TILES
            nc.vector.tensor_tensor(
                out=w_bf[grp][:],
                in0=weights[grp][:],
                in1=mask_t[c][:].unsqueeze(1).to_broadcast([P, width, W]),
                op=ALU.mult,
            )

        def quant_w(grp):
            width = grp[1] - grp[0]
            w_codes[grp] = flow.tile([P, width * QT], U32, name="w_codes", align_bytes=64, bufs=PENDING)
            w_scales[grp] = flow.tile([P, width * QT], U8, name="w_scales", align_bytes=64, bufs=PENDING)
            quantize(w_codes[grp][:], w_scales[grp][:], w_bf[grp][:].rearrange("p i x -> p (i x)"))

        def y_of(n):
            return y_bank[n % 2 if n >= UNITS - 2 else (n // SET) % Y_BANKS]

        def attend(grp):
            for n in range(*grp):
                s, g = divmod(n, SET)
                a = s // TILES
                cols = slice(QT * (n - grp[0]), QT * (n - grp[0] + 1))
                nc.tensor.matmul_mx(
                    out=y_of(n)[:, g, :],
                    lhsT=w_codes[grp][:, cols].bitcast(FP8X4),
                    lhsT_scale=w_scales[grp][:, cols],
                    rhs=v_codes[a][:, D * g : D * (g + 1)].bitcast(FP8X4),
                    rhs_scale=v_scales[a][:, D * g : D * (g + 1)],
                    start=True,
                    stop=True,
                )

        def gate_y(s, g0=0, g1=SET):
            y = y_of(SET * s + g0)
            nc.vector.reciprocal(out=recip[s][:, g0:g1], in_=y[:, g0:g1, D - 1])
            nc.vector.scalar_tensor_tensor(
                out=result[s][:, g0:g1, :],
                in0=gate[s][:, g0:g1, :],
                scalar=1.0,
                in1=y[:, g0:g1, :],
                op0=ALU.add,
                op1=ALU.mult,
            )

        def finish(s, g0=0, g1=SET, queue=nc.sync):
            for g in range(g0, g1):
                nc.vector.tensor_scalar(
                    out=result[s][:, g, :],
                    in0=result[s][:, g, :],
                    scalar1=recip[s][:, g : g + 1],
                    scalar2=0.5,
                    op0=ALU.mult,
                    op1=ALU.mult,
                )
            queue.dma_start(out=rows_of(out, s, g0, g1), in_=result[s][:, g0:g1, :])

        def finish_on_scalar(s, g0=0, g1=SET):
            nc.scalar.mul(out=half_recip[s][:, g0:g1], in_=recip[s][:, g0:g1], mul=0.5)
            for g in range(g0, g1):
                nc.scalar.activation(out=result[s][:, g, :], in_=result[s][:, g, :], func=ACT.Copy, scale=half_recip[s][:, g : g + 1])
            nc.sync.dma_start(out=rows_of(out, s, g0, g1), in_=result[s][:, g0:g1, :])

        spread_k(0, 0, 0, 2)
        spread_k(0, 1, 0, 2)
        spread_k(0, 0, 2, PACK, nc.scalar.copy)
        spread_k(0, 1, 2, PACK)
        spread_q(0, 0, 1)
        quant_k(0, 0, HALF)
        quant_q(0, 0, 1)
        quant_k(0, HALF, N)
        gate_tanh(0)
        scores([0, 1])
        scores([2, 3])
        spread_q(0, 1, 2)
        quant_q(0, 1, 2)
        scale_mask(m01)
        spread_mask(0)
        spread_mask(1)
        spread_v(0, 0)
        cap(0)

        before = {grp[0]: [] for grp in groups}
        after = {grp[0]: [] for grp in groups}
        operands = [
            ([(spread_q, 0, 2, TILES)], [(quant_q, 0, 2, TILES)]),
            ([(spread_v, 0, 1)], [(quant_v, 0)]),
            ([(scale_mask, m23)], [(spread_mask, 2), (spread_mask, 3)]),
            ([(spread_k, 1, 0, 0, PACK)], [(spread_k, 1, 1, 0, PACK)]),
            ([(quant_k, 1, 0, N)], [(spread_q, 1, 0, 2)]),
            ([(quant_q, 1, 0, 2), (spread_q, 1, 2, TILES)], [(quant_q, 1, 2, TILES)]),
            ([(spread_v, 1, 0)], [(spread_v, 1, 1)]),
        ]
        for grp, (jobs_before, jobs_after) in zip(groups, operands):
            before[grp[0]].extend(jobs_before)
            after[grp[0]].extend(jobs_after)
        before[FIRST_GATED + 2].append((quant_v, 1))
        last = STEPS - 1
        gate_at = {}
        for s in range(last):
            n = max(FIRST_GATED + 2 * s, SET * (s + 1))
            before[n].append((gate_y, s))
            if n > SET * (s + 1):
                after[n].append((finish, s))
            elif s < last - 1:
                before[n + 2].append((finish, s))
            if s > 0:
                gate_at[n - GATE_LEAD if s < last - 1 else n] = s

        capped_upto = 1
        waiting = []
        for grp in groups[:-2]:
            for n in range(capped_upto, grp[1] + 1):
                cap(n)
            capped_upto = grp[1] + 1
            if grp[0] in gate_at:
                gate_tanh(gate_at[grp[0]])
            exponent(grp)
            if grp[0] % SET == 0:
                for done in waiting:
                    attend(done)
                waiting = []
            weigh(grp)
            for job in before[grp[0]]:
                job[0](*job[1:])
            quant_w(grp)
            waiting.append(grp)
            for job in after[grp[0]]:
                job[0](*job[1:])

        cap(UNITS - 1)
        exponent(groups[-2])
        exponent(groups[-1])
        gate_tanh(last)
        finish_on_scalar(last - 1)
        for done in waiting:
            attend(done)
        weigh(groups[-2])
        weigh(groups[-1])
        for grp in groups[-2:]:
            quant_w(grp)
            attend(grp)
        gate_y(last, 0, 2)
        finish_on_scalar(last, 0, 2)
        gate_y(last, 2, 3)
        gate_y(last, 3, SET)
        finish(last, 2, 3)
        finish(last, 3, SET, nc.scalar)
